import numpy as np
CORES = [3,5,19,21,35,37,51,53,67,69]
N = 10
T, FF, CAP, CAPP = 4096, 3, 1120, 224
def entries(a): return a.T.reshape(-1)
def pack(v, P): return np.ascontiguousarray(np.asarray(v, np.int32).reshape(-1, P).T)
def lists(rng, how):
    O = np.stack([rng.permutation(np.repeat(np.arange(N), CAPP))[:CAP] for k in range(N)])
    if how == "apart": s = int(rng.integers(N * CAPP - CAP + 1)); cnt = np.bincount(np.repeat(np.arange(N), CAPP)[s:s + CAP], minlength=N); a = rng.permutation(N); O = np.stack([rng.permutation(np.repeat(np.arange(N), cnt[(a + k) % N])) for k in rng.permutation(N)])
    if how == "full": z = rng.permutation(N); O = np.stack([rng.permutation(np.repeat(z, CAPP)[:CAP]) for k in range(N)])
    if how == "none": z = int(rng.integers(N)); O = np.stack([rng.permutation(np.repeat(np.delete(np.arange(N), z), CAPP))[:CAP] for k in range(N)])
    P = np.zeros((N, CAP), np.int64)
    for o in range(N):
        q = rng.permutation(T); u = 0
        for k in range(N):
            m = np.nonzero(O[k] == o)[0]
            if how != "apart": q = rng.permutation(T); u = 0
            if how == "sorted": q = np.r_[0, T - 1, 1 + rng.permutation(T - 2)]
            P[k, m] = T * o + q[u:u + len(m)]; u += len(m)
    if how == "same": P = np.stack([rng.permutation(P[0]) for k in range(N)])
    if how == "sorted": P = np.sort(P, axis=1)
    G = 2 * rng.random((N, 16, CAP // 16), dtype=np.float32) - 1
    if how == "none": G[rng.random(G.shape) < 0.125] = 0
    return {"gate": G, "pick": np.stack([pack(p, 16) for p in P])}
def setup_inputs(rng):
    return dict({"x": rng.standard_normal((N, 128, T), dtype=np.float32), "w1": (rng.standard_normal((N, 128, FF * 128), dtype=np.float32) / 8), "w2": (rng.standard_normal((N, 128, FF * 128), dtype=np.float32) / 16)}, **lists(rng, "uniform"))
def setup_inputs_apart(rng):
    d = setup_inputs(rng); d.update(lists(rng, "apart"))
    for k in ("x",): d[k] = (d[k].astype(np.float32) * 1024.0).astype(d[k].dtype)
    return d
def setup_inputs_full(rng):
    d = setup_inputs(rng); d.update(lists(rng, "full"))
    for k in ("x",): d[k] = (d[k].astype(np.float32) * (1 / 1024.0)).astype(d[k].dtype)
    return d
def setup_inputs_none(rng):
    d = setup_inputs(rng); d.update(lists(rng, "none"))
    return d
def setup_inputs_same(rng):
    d = setup_inputs(rng); d.update(lists(rng, "same"))
    return d
def setup_inputs_sorted(rng):
    d = setup_inputs(rng); d.update(lists(rng, "sorted"))
    return d
def check_inputs(x):
    bad = []
    if x["pick"].min() < 0 or x["pick"].max() >= N * T: bad.append("pick out of range")
    if any(len(np.unique(a)) != a.size for a in x["pick"]): bad.append("a token stands twice in a list")
    if max(int(np.bincount(entries(a) // T, minlength=N).max()) for a in x["pick"]) > CAPP: bad.append("more than CAPP of an expert's tokens lie on one rank")
    return bad
def reference(x, w1, w2, gate, pick):
    X, W1, W2 = x.astype(np.float64), w1.astype(np.float64), w2.astype(np.float64)
    A = np.concatenate(list(X), axis=1); Y = np.zeros((128, N * T))
    for k in range(N):
        P = entries(pick[k]); g = entries(gate[k]).astype(np.float64)
        Y[:, P] += g[None, :] * sum(W2[k][:, 128 * f:128 * f + 128].T @ np.maximum(W1[k][:, 128 * f:128 * f + 128].T @ A[:, P], 0.0) for f in range(FF))
    return {"y": np.stack([Y[:, T * r:T * r + T] for r in range(N)]).astype(np.float32)}

@@ -1,0 +1,391 @@
+from concourse.bass import DstId, RemoteDMATransfer
+from concourse.mybir import AluOpType, ActivationFunctionType
+
+TOK, FF = 4096, 3
+HC = 112
+PADC = TOK + 224
+XC = 2048
+
+F, B, I, U = "float32", "bfloat16", "int32", "uint16"
+SCRATCH = {name: ("sbuf", [p, w], ty) for name, p, w, ty in (
+    ("picki", 128, 10, I), ("gatef", 128, 10, F), ("pk", 128, 20, F), ("pkr", 128, 20, F),
+    ("w1b", 128, 384, F), ("w2b", 128, 384, F), ("wf1", 128, 384, F), ("wf2", 128, 384, F),
+    ("xb", 128, PADC, F), ("yb", 128, PADC, F), ("tks", 128, 2240, F), ("tin", 128, 448, F), ("trl", 128, 448, F),
+    ("hid", 128, 1344, F), ("res", 128, 448, F), ("rs", 128, 2240, F), ("tmp", 128, 224, F), ("lst", 128, 160, U),
+    ("llist", 128, 32, U), ("im", 128, 128, B), ("i32", 128, 32, B), ("imf", 128, 224, F), ("pcol", 128, 1, I),
+    ("pm", 128, 1, I), ("pmf", 128, 1, F), ("mask", 128, 224, F), ("sel", 16, 128, B), ("padlo", 16, 32, B),
+    ("padhi", 16, 32, B), ("ones", 128, 128, B), ("tri", 128, 128, B), ("ones16", 16, 128, F), ("exi", 128, 14, I),
+    ("exu", 128, 14, U), ("rst", 128, 20, B), ("gm", 128, 30, B), ("m", 128, 20, B), ("scn", 128, 20, B), ("m4", 128, 20, B),
+    ("qf", 128, 20, F), ("fs", 128, 80, F), ("kv", 128, 20, I), ("dq", 128, 30, I), ("dqf", 128, 30, F), ("lb", 128, 1280, B),
+    ("rb", 128, 640, B), ("rg", 128, 960, B), ("gb", 128, 30, B), ("gbf", 128, 30, F), ("gw", 128, 32, F), ("eg", 128, 448, F),
+    ("gsb", 128, 448, F))}
+SCRATCH.update({"p%d" % b: ("psum", [128, 512], F) for b in range(8)})
+SEMAPHORES = (["ldp", "ldx", "yo", "gx", "vs", "ss", "ts", "gs", "sent", "pks", "pkrs", "w1s", "w2s", "f1s", "f2s", "tk0", "tk1", "trs"]
+              + ["l%d" % e for e in range(10)] + ["r%d" % e for e in range(10)])
+
+GATHER_V, GATHER_S = [0, 2, 4, 8, 6], [1, 3, 5, 9, 7]
+COMBINE = {True: [0, 2, 4, 1, 3, 5, 8, 9, 6, 7],
+           False: [0, 2, 4, 1, 3, 5, 6, 7, 8, 9]}
+
+
+def plan(cores, topo):
+    sims = range(80)
+    chips = []
+    for c in cores:
+        if topo.chip(c) not in chips:
+            chips.append(topo.chip(c))
+    rank = [[c for c in cores if topo.chip(c) == ch] for ch in chips]
+    relay, jobs = [], {}
+    for i, ch in enumerate(chips):
+        mcore = [c for c in sims if topo.mates(ch, topo.chip(c))]
+        relay.append([])
+        for s in (0, 1):
+            rc = rank[i][s]
+            h = [c for c in sims if topo.chip(c) == ch and topo.die(c) == topo.die(rc) and c != rc]
+            h.sort(key=lambda c: (topo.may_write(c, mcore[0]), c))
+            back = [c for c in mcore if topo.die(c) == topo.die(rc) and topo.may_write(c, rc)]
+            relay[i].append(None if topo.may_write(rc, mcore[0]) else h[1])
+            for r, c in enumerate([rc] + h[:3] + back[:1]):
+                jobs[i, s, r] = c
+    return rank, relay, jobs, len(chips)
+
+
+def rank_program(g, core, T, topo):
+    A, AF, S = AluOpType, ActivationFunctionType, T.sem
+    rank, relay, jobs, n = plan(T.cores, topo)
+    mine = [k for k in jobs if jobs[k] == core]
+    if not mine:
+        return
+    i, s, r = mine[0]
+    is_rank = r == 0
+    a0 = TOK * T.cores.index(rank[i][0])
+    Qs = {"v": g.vector, "s": g.scalar, "t": g.tensor, "g": g, "y": g.sync}
+    v, tt, ts, mm = g.vector, g.vector.tensor_tensor, g.vector.tensor_scalar, g.tensor.matmul
+    cnt, seen = {}, {}
+    order = [s, 1 - s]
+    if r == 4:
+        order.sort(key=lambda x: relay[i][x] is not None)
+
+    def bump(sem, k=1):
+        cnt[sem] = cnt.get(sem, 0) + k
+        return cnt[sem]
+
+    def wait(q, sem, val=None):
+        val = cnt[sem] if val is None else val
+        if seen.get((q, sem), 0) < val:
+            Qs[q].wait_ge(S[sem], val)
+            seen[q, sem] = val
+
+    def V(ins):
+        ins.then_inc(S.vs, 1)
+        return bump("vs")
+
+    def SC(ins):
+        ins.then_inc(S.ss, 1)
+        return bump("ss")
+
+    def PE(ins):
+        ins.then_inc(S.ts, 1)
+        return bump("ts")
+
+    def GP(ins):
+        ins.then_inc(S.gs, 1)
+        return bump("gs")
+
+    def bits(mask):
+        return bin(mask).count("1")
+
+    def split(mask, k):
+        b = [e for e in range(16) if mask >> e & 1]
+        w = len(b) // k
+        return [sum(1 << e for e in b[j * w:(j + 1) * w]) for j in range(k)]
+
+    def send(*trs):
+        out = []
+        for src, dst, sem, dsts, mask in trs:
+            ids = [DstId(rid=topo.addr(d)[0], pnc=topo.addr(d)[1]) for d in dsts]
+            out.append(RemoteDMATransfer(dst_ids=ids, dma_engine_mask=mask, remote_sem=S[sem], srcs=[src], dsts=[dst] * len(ids)))
+            bump("sent", bits(mask))
+        g.remote_dma_fused(out, local_sem=S.sent)
+
+    def place(x, sj, rr):
+        return 2 * rr + (1 if sj != x else 0)
+
+    def half(t, x, w=224):
+        return t[:, w * x:w * x + w]
+
+    allm = topo.mask(rank[0][0], rank[0][1])
+    offm = topo.mask(rank[0][0], rank[1][0])
+    restm = allm & ~offm
+
+    if is_rank:
+        g.sync.dma_start(T.picki[0:HC, :], T.pick[:]).then_inc(S.ldp, 16)
+        g.scalar.dma_start(T.gatef[0:HC, :], T.gate[:]).then_inc(S.ldp, 16)
+        g.sync.dma_start(T.picki[HC:128, :], T.pick[:, 0:10]).then_inc(S.ldp, 16)
+        g.scalar.dma_start(T.gatef[HC:128, :], T.gate[:, 0:10]).then_inc(S.ldp, 16)
+        g.sync.dma_start(T.w1b[:], T.w1[:]).then_inc(S.w1s, 16)
+        g.sync.dma_start(T.w2b[:], T.w2[:]).then_inc(S.w2s, 16)
+
+    c_ones = V(v.memset(T.ones[:], 1.0))
+    c_rst = V(v.memset(T.rst[:], 1.0))
+    V(v.memset(T.padhi[:], float(TOK)))
+    V(v.memset(T.ones16[:], 1.0))
+    wait("v", "vs", c_rst)
+    V(v.memset(T.rst[:, 10:11], 0.0))
+    if is_rank:
+        V(v.memset(T.xb[:, TOK:PADC], 0.0))
+    GP(g.iota(T.im[:], [[0, 8], [1, 16]], 0, 0, allow_small_or_imprecise_dtypes=True))
+    g_p = GP(g.iota(T.pcol[:], [[0, 1]], 0, 1))
+    GP(g.iota(T.padlo[:], [[0, 2], [16, 16]], 0, 1, allow_small_or_imprecise_dtypes=True))
+    wait("g", "vs", c_ones)
+    g_tri = GP(g.affine_select(T.tri[:], T.ones[:], [[1, 128]], A.is_gt, 0.0, 0, -1))
+    g_i32 = GP(g.iota(T.i32[:], [[1, 32]], 0, 0, allow_small_or_imprecise_dtypes=True))
+    GP(g.iota(T.imf[:], [[0, 14], [1, 16]], 0, 0, allow_small_or_imprecise_dtypes=True))
+    g_all = GP(g.iota(T.exi[:], [[1, 14]], 0, 0))
+    wait("v", "gs", g_p)
+    k = V(ts(T.pm[:], T.pcol[:], 15, None, A.bitwise_and))
+    wait("v", "vs", k)
+    k = V(v.tensor_copy(T.pmf[:], T.pm[:]))
+    wait("v", "vs", k)
+    V(ts(T.sel[:], T.im[0:16, :], T.pmf[0:16, :], None, A.is_equal))
+
+    if is_rank:
+        wait("v", "ldp", 64)
+        V(v.tensor_copy(T.pk[:, 0:10], T.picki[:]))
+        k = V(v.tensor_copy(T.pk[:, 10:20], T.gatef[:]))
+        wait("v", "vs", k)
+        far = [jobs[(i + rr) % n, s, rr] for rr in range(1, 5)]
+        direct = [d for d in far if topo.may_write(core, d)]
+        f1, f2 = jobs[i, s, 3], jobs[i, s, 1]
+        wait("g", "vs", k)
+        trs = [(T.pk[:], T.pk[:], "pks", direct, offm)]
+        if len(direct) < len(far):
+            trs.append((T.pk[:], T.pkr[:], "pkrs", [f1], restm))
+        send(*trs)
+        wait("g", "w1s", 16)
+        send((T.w1b[:], T.wf1[:], "f1s", [f1], allm))
+        wait("g", "w2s", 16)
+        send((T.w2b[:], T.wf2[:], "f2s", [f2, f1], allm))
+        g.sem_inc(S.gx, 1)
+        wait("y", "gx", 1)
+        for c in range(0, TOK, XC):
+            g.sync.dma_start(T.xb[:, c:c + XC], T.x[:, c:c + XC]).then_inc(S.ldx, 16)
+    else:
+        wait("v", "pks", bits(offm))
+    n_w = 16 if is_rank else bits(offm)
+
+    def R(t, a=0, b=10):
+        return t[0:HC, a:b]
+
+    u1, t1, ka, kb, vhi, r1, r2 = [R(T.fs, 10 * j, 10 * j + 10) for j in range(7)]
+    ki, vi, tok = R(T.kv, 0, 10), R(T.kv, 10, 20), R(T.pk)
+    for j in range(3):
+        k = V(ts(R(T.gm, 10 * j, 10 * j + 10), tok, float(a0 + TOK * j), None, A.is_ge))
+    wait("v", "vs", k)
+    k = V(tt(R(T.m, 0, 20), R(T.gm, 0, 20), R(T.gm, 10, 30), A.subtract))
+    wait("v", "vs", k)
+    k_scn = V(v.tensor_tensor_scan(R(T.scn, 0, 20), R(T.rst, 0, 20), R(T.m, 0, 20), 0.0, A.mult, A.add))
+    wait("t", "gs", g_tri)
+    wait("t", "vs", k_scn)
+    t_base = PE(mm(T.p3[0:HC, 0:2], T.tri[0:HC, 0:HC], T.scn[0:HC, 9:20:10], True, True))
+    PE(mm(T.p7[:, 0:32], T.sel[:], T.padhi[:], True, False))
+    PE(mm(T.p7[:, 0:32], T.sel[:], T.padlo[:], False, False))
+    k_m4 = V(ts(R(T.m4, 0, 20), R(T.m, 0, 20), 4096.0, None, A.mult))
+    V(ts(u1, R(T.gm, 10, 20), -3840.0, float(-(a0 + TOK)), A.mult, A.add))
+    wait("v", "vs", k_m4)
+    V(tt(R(T.qf, 0, 20), R(T.scn, 0, 20), R(T.m4, 0, 20), A.add))
+    wait("v", "vs", k_m4 + 1)
+    k = V(tt(t1, tok, u1, A.add))
+    wait("v", "vs", k)
+    wait("v", "ts", t_base)
+    V(ts(ka, R(T.qf, 0, 10), T.p3[0:HC, 0:1], -4097.0, A.add, A.add))
+    k_base = V(ts(kb, R(T.qf, 10, 20), T.p3[0:HC, 1:2], -3841.0, A.add, A.add))
+    wait("v", "vs", k_base)
+    k = V(tt(ki, ka, kb, A.max))
+    wait("v", "vs", k)
+    V(ts(R(T.dq, 10, 20), ki, 15, None, A.bitwise_and))
+    V(ts(R(T.dq, 0, 10), ki, 4, None, A.arith_shift_right))
+    k = V(tt(vi, t1, ki, A.subtract))
+    wait("v", "vs", k)
+    k = V(ts(R(T.dq, 20, 30), vi, 63, None, A.bitwise_and))
+    wait("v", "vs", k)
+    k = V(v.tensor_copy(R(T.dqf, 0, 30), R(T.dq, 0, 30)))
+    wait("v", "vs", k)
+    k_vhi = V(tt(vhi, vi, R(T.dqf, 20, 30), A.subtract))
+    wait("v", "gs", g_i32)
+    for c in range(10):
+        lh = T.lb[0:HC, 128 * c:128 * c + 128]
+        lo, hi = T.rb[0:HC, 64 * c:64 * c + 32], T.rb[0:HC, 64 * c + 32:64 * c + 64]
+        V(ts(lh, T.im[0:HC, :], T.dqf[0:HC, 10 + c:11 + c], None, A.is_equal))
+        k = V(ts(lo, T.i32[0:HC, :], T.dqf[0:HC, c:c + 1], T.dqf[0:HC, 20 + c:21 + c], A.is_equal, A.mult))
+        wait("t", "vs", k)
+        PE(mm(T.p7[:, 0:32], lh, lo, False, False))
+        wait("v", "vs", k_vhi)
+        k = V(ts(hi, T.i32[0:HC, :], T.dqf[0:HC, c:c + 1], T.fs[0:HC, 40 + c:41 + c], A.is_equal, A.mult))
+        wait("t", "vs", k)
+        k = PE(mm(T.p7[:, 0:32], lh, hi, False, c == 9))
+    wait("v", "ts", k)
+    k_list = V(v.tensor_copy(T.llist[:], T.p7[:, 0:32]))
+    n_l = [0, bits(allm)] + [bits(offm) // 2] * 8
+
+    if r == 3:
+        dst = [jobs[(i + rr) % n, s, rr] for rr in (1, 4, 2, 3)]
+        if not topo.may_write(rank[i][s], dst[1]):
+            wait("g", "pkrs", bits(restm))
+            send((T.pkr[:], T.pk[:], "pks", [dst[1]], offm))
+        wait("g", "f1s", bits(allm))
+        send((T.wf1[:], T.w1b[:], "w1s", [dst[0]], offm))
+        send((T.wf1[:], T.w1b[:], "w1s", [dst[1]], offm))
+        wait("g", "f2s", bits(allm))
+        send((T.wf2[:], T.w2b[:], "w2s", [dst[1]], offm))
+        send((T.wf1[:], T.w1b[:], "w1s", [dst[2]], offm))
+        send((T.wf1[:], T.w1b[:], "w1s", [dst[3]], offm))
+    if r == 1:
+        wait("g", "f2s", bits(allm))
+        for rr in (1, 2, 3):
+            send((T.wf2[:], T.w2b[:], "w2s", [jobs[(i + rr) % n, s, rr]], offm))
+    wait("g", "vs", k_list)
+    mk = split(offm if r == 4 else restm, 2)
+    trs = []
+    for x in order:
+        e = place(x, s, r)
+        if e:
+            trs.append((T.llist[:, 16 * x:16 * x + 16], T.lst[:, 16 * e:16 * e + 16], "l%d" % e, [rank[i][x]],
+                        allm if is_rank else mk[len(trs)]))
+    send(*trs)
+    for x in (0, 1):
+        if relay[i][x] == core:
+            mk = split(offm, 2)
+            wait("g", "trs", bits(allm))
+            send(*[(half(T.trl, j), half(T.tin, x), "tk%d" % x, [jobs[i, (x, 1 - x)[j], 4]], mk[j]) for j in (0, 1)])
+
+    wait("v", "gs", g_all)
+    V(ts(T.mask[:], T.imf[:], T.pmf[:], None, A.is_equal))
+    V(v.tensor_copy(T.exu[:], T.exi[:]))
+    gate, g1, g2, g3 = R(T.pk, 10, 20), R(T.gb, 0, 10), R(T.gb, 10, 20), R(T.gb, 20, 30)
+    for out, a, b in ((g1, gate, None), (r1, gate, g1), (g2, r1, None), (r2, r1, g2), (g3, r2, None),
+                      (R(T.gbf, 0, 30), R(T.gb, 0, 30), None)):
+        k = V(v.tensor_copy(out, a) if b is None else tt(out, a, b, A.subtract))
+        wait("v", "vs", k)
+    for c in range(10):
+        for j in range(3):
+            o = 96 * c + 32 * j
+            k = V(ts(T.rg[0:HC, o:o + 32], T.i32[0:HC, :], T.dqf[0:HC, c:c + 1], T.gbf[0:HC, 10 * j + c:10 * j + c + 1],
+                     A.is_equal, A.mult))
+        wait("t", "vs", k)
+        for j in range(3):
+            o = 96 * c + 32 * j
+            k = PE(mm(T.p6[:, 0:32], T.lb[0:HC, 128 * c:128 * c + 128], T.rg[0:HC, o:o + 32], c == 0 and j == 0, c == 9 and j == 2))
+    wait("v", "ts", k)
+    k_gw = V(v.tensor_copy(T.gw[:], T.p6[:, 0:32]))
+    wait("v", "vs", k_gw)
+    for x in (0, 1):
+        k = V(tt(half(T.eg, x), T.gw[:, 16 * x:16 * x + 14].indirect(T.exu[:]), T.mask[:], A.mult))
+    wait("t", "vs", k)
+    k = PE(mm(T.p5[:, 0:448], T.ones16[:], T.eg[0:16, :], True, True))
+    wait("s", "ts", k)
+    k_gsb = SC(g.scalar.activation(T.gsb[:], T.p5[:, 0:448], AF.Copy))
+
+    got = {}
+
+    def lst(e):
+        return T.llist[:, 16 * s:16 * s + 14] if e == 0 else T.lst[:, 16 * e:16 * e + 14]
+
+    def gather(q, e):
+        wait(q, "ldx", 16 * (TOK // XC))
+        wait(q, "vs", k_list)
+        if e:
+            wait(q, "l%d" % e, n_l[e])
+        out = half(T.tks, e) if e else half(T.tin, s)
+        if q == "v":
+            got[e] = ("vs", V(v.tensor_copy(out, T.xb[:].indirect(lst(e)))))
+        else:
+            got[e] = ("ss", SC(g.scalar.activation(out, T.xb[:].indirect(lst(e)), AF.Copy)))
+
+    if is_rank:
+        V(v.memset(T.yb[:], 0.0))
+        for e in GATHER_V:
+            gather("v", e)
+        for e in GATHER_S:
+            gather("s", e)
+        for rr in (0, 1, 2, 4, 3):
+            mk = split(allm, 2)
+            if rr == 0:
+                wait("g", *got[1])
+                send((half(T.tks, 1), half(T.tin, s), "tk%d" % s, [rank[i][1 - s]], mk[0]))
+                continue
+            for e in (2 * rr, 2 * rr + 1):
+                wait("g", *got[e])
+            if rr == 4:
+                if relay[i][s] is not None:
+                    send((T.tks[:, 8 * 224:10 * 224], T.trl[:], "trs", [relay[i][s]], allm))
+                    continue
+                mk = split(offm, 2)
+            send(*[(half(T.tks, 2 * rr + j), half(T.tin, s), "tk%d" % s, [jobs[i, (s, 1 - s)[j], rr]], mk[j]) for j in (0, 1)])
+
+    P = [T["p%d" % b] for b in range(8)]
+    hd = {}
+
+    def layer1(b, x):
+        wait("t", "w1s", n_w)
+        if is_rank and x == s:
+            wait("t", *got[0])
+        else:
+            wait("t", "tk%d" % x, bits(allm) // 2 if r < 4 else bits(offm) // 2)
+        for f in range(FF):
+            if b and f:
+                wait("t", *([("ss", k_gsb), ("vs", k_gw)][f - 1]))
+            hd[x, f] = PE(mm(P[4 * b + f][:, 0:224], T.w1b[:, 128 * f:128 * f + 128], half(T.tin, x), True, True))
+        for f in range(FF):
+            wait("s", "ts", hd[x, f])
+            o = 672 * b + 224 * f
+            hd[x, f] = SC(g.scalar.activation(T.hid[:, o:o + 224], P[4 * b + f][:, 0:224], AF.Relu))
+
+    def layer2(b, x):
+        wait("t", "w2s", n_w)
+        wait("t", "vs", k_list if b else k_base)
+        for f in range(FF):
+            wait("t", "ss", hd[x, f])
+            o = 672 * b + 224 * f
+            k = PE(mm(P[4 * b + 3][:, 0:224], T.w2b[:, 128 * f:128 * f + 128], T.hid[:, o:o + 224], f == 0, f == 2))
+        return k
+
+    def finish(b, x, k):
+        wait("v", "ts", k)
+        wait("v", "ss", k_gsb)
+        k = V(tt(half(T.res, x), P[4 * b + 3][:, 0:224], half(T.gsb, x), A.mult))
+        if not (is_rank and x == s):
+            wait("g", "vs", k)
+            e = place(x, s, r)
+            send((half(T.res, x), half(T.rs, e), "r%d" % e, [rank[i][x]], allm if r < 4 else offm))
+        return k
+
+    layer1(0, order[0])
+    if r == 3:
+        layer1(1, order[1])
+        for b, x in enumerate(order):
+            finish(b, x, layer2(b, x))
+    else:
+        k_self = finish(0, order[0], layer2(0, order[0]))
+        layer1(1, order[1])
+        k = layer2(1, order[1])
+        if not is_rank:
+            finish(1, order[1], k)
+    if is_rank:
+        yall = T.yb[:]
+        wait("v", "vs", k_self)
+        ky = V(v.tensor_copy(yall.indirect(lst(0)), half(T.res, s)))
+        finish(1, 1 - s, k)
+        for e in COMBINE[relay[i][s] is None][1:]:
+            wait("v", "r%d" % e, bits(offm if e > 7 else allm))
+            wait("v", "vs", ky)
+            ky = V(tt(T.tmp[:], yall.indirect(lst(e)), half(T.rs, e), A.add))
+            wait("v", "vs", ky)
+            ky = V(v.tensor_copy(yall.indirect(lst(e)), T.tmp[:]))
+        for q in ("y", "s"):
+            wait(q, "vs", ky)
+        g.sync.dma_start(T.y[:, 0:2048], T.yb[:, 0:2048]).then_inc(S.yo, 16)
+        g.scalar.dma_start(T.y[:, 2048:4096], T.yb[:, 2048:4096]).then_inc(S.yo, 16)
+        wait("g", "yo", 32)
+    for sem in ("vs", "ss", "ts", "gs", "sent"):
+        wait("g", sem)

@@ -4,7 +4,10 @@ from concourse.mybir import AluOpType, ActivationFunctionType
 TOK, FF = 4096, 3
 HC = 112
 PADC = TOK + 224
-XC = 2048
+XC = [0, 512, 2304, 4096]
+YP = 432
+FIN = 2
+HI = {4: (0, 1), 5: (2, 3), 6: (4, 5), 7: (6, 7), 8: (8,), 9: (9,)}
 
 F, B, I, U = "float32", "bfloat16", "int32", "uint16"
 SCRATCH = {name: ("sbuf", [p, w], ty) for name, p, w, ty in (
@@ -16,16 +19,16 @@ SCRATCH = {name: ("sbuf", [p, w], ty) for name, p, w, ty in (
     ("pm", 128, 1, I), ("pmf", 128, 1, F), ("mask", 128, 224, F), ("sel", 16, 128, B), ("padlo", 16, 32, B),
     ("padhi", 16, 32, B), ("ones", 128, 128, B), ("tri", 128, 128, B), ("ones16", 16, 128, F), ("exi", 128, 14, I),
     ("exu", 128, 14, U), ("rst", 128, 20, B), ("gm", 128, 30, B), ("m", 128, 20, B), ("scn", 128, 20, B), ("m4", 128, 20, B),
-    ("qf", 128, 20, F), ("fs", 128, 80, F), ("kv", 128, 20, I), ("dq", 128, 30, I), ("dqf", 128, 30, F), ("lb", 128, 1280, B),
-    ("rb", 128, 640, B), ("rg", 128, 960, B), ("gb", 128, 30, B), ("gbf", 128, 30, F), ("gw", 128, 32, F), ("eg", 128, 448, F),
-    ("gsb", 128, 448, F))}
+    ("qf", 128, 20, F), ("fs", 128, 90, F), ("kv", 128, 20, I), ("dq", 128, 30, I), ("dqf", 128, 30, F), ("lb", 128, 1280, B),
+    ("ab", 128, 320, B), ("rb", 128, 640, B), ("rg", 128, 960, B), ("gb", 128, 30, B), ("gbf", 128, 30, F), ("gw", 128, 32, F),
+    ("eg", 128, 448, F), ("gsb", 128, 448, F))}
 SCRATCH.update({"p%d" % b: ("psum", [128, 512], F) for b in range(8)})
-SEMAPHORES = (["ldp", "ldx", "yo", "gx", "vs", "ss", "ts", "gs", "sent", "pks", "pkrs", "w1s", "w2s", "f1s", "f2s", "tk0", "tk1", "trs"]
-              + ["l%d" % e for e in range(10)] + ["r%d" % e for e in range(10)])
+SEMAPHORES = (["ldp", "ldx", "yo", "gx", "vs", "ss", "ts", "gs", "sent", "pks", "pkrs", "w1s", "w2s", "f1s", "f2s", "tk0", "tk1",
+               "tr0", "tr1", "gts"] + ["l%d" % e for e in range(10)] + ["r%d" % e for e in range(10)])
 
-GATHER_V, GATHER_S = [0, 2, 4, 8, 6], [1, 3, 5, 9, 7]
-COMBINE = {True: [0, 2, 4, 1, 3, 5, 8, 9, 6, 7],
-           False: [0, 2, 4, 1, 3, 5, 6, 7, 8, 9]}
+GATHER_V, GATHER_S = [0, 2, 4, 6], [1, 3, 5, 7]
+COMBINE = {True: [0, 2, 4, 1, 6, 8, 3, 5, 7, 9],
+           False: [0, 2, 4, 1, 6, 3, 5, 9, 7, 8]}
 
 
 def plan(cores, topo):
@@ -45,7 +48,7 @@ def plan(cores, topo):
             h.sort(key=lambda c: (topo.may_write(c, mcore[0]), c))
             back = [c for c in mcore if topo.die(c) == topo.die(rc) and topo.may_write(c, rc)]
             relay[i].append(None if topo.may_write(rc, mcore[0]) else h[1])
-            for r, c in enumerate([rc] + h[:3] + back[:1]):
+            for r, c in enumerate([rc] + h[:3] + back[:2]):
                 jobs[i, s, r] = c
     return rank, relay, jobs, len(chips)
 
@@ -57,21 +60,21 @@ def rank_program(g, core, T, topo):
     if not mine:
         return
     i, s, r = mine[0]
-    is_rank = r == 0
+    is_rank, second = r == 0, r == 5
+    r = min(r, 4)
     a0 = TOK * T.cores.index(rank[i][0])
     Qs = {"v": g.vector, "s": g.scalar, "t": g.tensor, "g": g, "y": g.sync}
-    v, tt, ts, mm = g.vector, g.vector.tensor_tensor, g.vector.tensor_scalar, g.tensor.matmul
+    v, tt, ts, mm, act = g.vector, g.vector.tensor_tensor, g.vector.tensor_scalar, g.tensor.matmul, g.scalar.activation
     cnt, seen = {}, {}
     order = [s, 1 - s]
-    if r == 4:
-        order.sort(key=lambda x: relay[i][x] is not None)
+    lates = sorted((0, 1), key=lambda sj: relay[i][sj] is not None)
 
     def bump(sem, k=1):
         cnt[sem] = cnt.get(sem, 0) + k
         return cnt[sem]
 
     def wait(q, sem, val=None):
-        val = cnt[sem] if val is None else val
+        val = cnt.get(sem, 0) if val is None else val
         if seen.get((q, sem), 0) < val:
             Qs[q].wait_ge(S[sem], val)
             seen[q, sem] = val
@@ -111,12 +114,65 @@ def rank_program(g, core, T, topo):
     def place(x, sj, rr):
         return 2 * rr + (1 if sj != x else 0)
 
+    def doer(sj, rr, x):
+        return jobs[i, sj, rr if rr < 4 or x == sj else 5]
+
     def half(t, x, w=224):
         return t[:, w * x:w * x + w]
 
     allm = topo.mask(rank[0][0], rank[0][1])
     offm = topo.mask(rank[0][0], rank[1][0])
     restm = allm & ~offm
+    n_w = 16 if is_rank else bits(allm) if second else bits(offm)
+    n_l = [0, bits(allm)] + [bits(offm) // 2] * 8
+
+    P = [T["p%d" % b] for b in range(8)]
+    hd, got, mark = {}, {}, {}
+
+    def layer1(b, x):
+        wait("t", "w1s", n_w)
+        if is_rank and x == s:
+            wait("t", *got[0])
+        else:
+            wait("t", "tk%d" % x, bits(allm) // 2 if r < 4 else bits(offm))
+        for f in range(FF):
+            if b and f:
+                wait("t", *([("ss", mark["gsb"]), ("vs", mark["gw"])][f - 1]))
+            hd[x, f] = PE(mm(P[4 * b + f][:, 0:224], T.w1b[:, 128 * f:128 * f + 128], half(T.tin, x), True, True))
+        for f in range(FF):
+            wait("s", "ts", hd[x, f])
+            o = 672 * b + 224 * f
+            hd[x, f] = SC(act(T.hid[:, o:o + 224], P[4 * b + f][:, 0:224], AF.Relu))
+
+    def layer2(b, x):
+        wait("t", "w2s", n_w)
+        if not second:
+            wait("t", "vs", mark["list"] if b else mark["base"])
+        for f in range(FF):
+            wait("t", "ss", hd[x, f])
+            o = 672 * b + 224 * f
+            k = PE(mm(P[4 * b + 3][:, 0:224], T.w2b[:, 128 * f:128 * f + 128], T.hid[:, o:o + 224], f == 0, f == 2))
+        return k
+
+    def finish(b, x, k):
+        wait("v", "ts", k)
+        if second:
+            wait("v", "gts", bits(allm))
+        else:
+            wait("v", "ss", mark["gsb"])
+        k = V(tt(half(T.res, x), P[4 * b + 3][:, 0:224], half(T.gsb, x), A.mult))
+        if not (is_rank and x == s):
+            wait("g", "vs", k)
+            e = place(x, s, r)
+            send((half(T.res, x), half(T.rs, e), "r%d" % e, [rank[i][x]], allm if r < 4 else offm))
+        return k
+
+    if second:
+        layer1(0, 1 - s)
+        finish(0, 1 - s, layer2(0, 1 - s))
+        for sem in ("vs", "ss", "ts", "sent"):
+            wait("g", sem)
+        return
 
     if is_rank:
         g.sync.dma_start(T.picki[0:HC, :], T.pick[:]).then_inc(S.ldp, 16)
@@ -125,23 +181,37 @@ def rank_program(g, core, T, topo):
         g.scalar.dma_start(T.gatef[HC:128, :], T.gate[:, 0:10]).then_inc(S.ldp, 16)
         g.sync.dma_start(T.w1b[:], T.w1[:]).then_inc(S.w1s, 16)
         g.sync.dma_start(T.w2b[:], T.w2[:]).then_inc(S.w2s, 16)
+        g.sync.dma_start(T.xb[:, XC[0]:XC[1]], T.x[:, XC[0]:XC[1]]).then_inc(S.ldx, 16)
 
     c_ones = V(v.memset(T.ones[:], 1.0))
     c_rst = V(v.memset(T.rst[:], 1.0))
-    V(v.memset(T.padhi[:], float(TOK)))
+    V(v.memset(T.padhi[:], -float(TOK)))
     V(v.memset(T.ones16[:], 1.0))
     wait("v", "vs", c_rst)
     V(v.memset(T.rst[:, 10:11], 0.0))
     if is_rank:
         V(v.memset(T.xb[:, TOK:PADC], 0.0))
+        k = V(v.memset(T.yb[:, 0:YP], 0.0))
+        wait("s", "vs", k)
+        c = YP
+        while c < PADC:
+            w = min(c, PADC - c)
+            k_y0 = SC(act(T.yb[:, c:c + w], T.yb[:, 0:w], AF.Copy))
+            wait("s", "ss", k_y0)
+            c += w
     GP(g.iota(T.im[:], [[0, 8], [1, 16]], 0, 0, allow_small_or_imprecise_dtypes=True))
     g_p = GP(g.iota(T.pcol[:], [[0, 1]], 0, 1))
-    GP(g.iota(T.padlo[:], [[0, 2], [16, 16]], 0, 1, allow_small_or_imprecise_dtypes=True))
+    GP(g.iota(T.padlo[:], [[0, 2], [-16, 16]], 0, -1, allow_small_or_imprecise_dtypes=True))
     wait("g", "vs", c_ones)
     g_tri = GP(g.affine_select(T.tri[:], T.ones[:], [[1, 128]], A.is_gt, 0.0, 0, -1))
     g_i32 = GP(g.iota(T.i32[:], [[1, 32]], 0, 0, allow_small_or_imprecise_dtypes=True))
-    GP(g.iota(T.imf[:], [[0, 14], [1, 16]], 0, 0, allow_small_or_imprecise_dtypes=True))
-    g_all = GP(g.iota(T.exi[:], [[1, 14]], 0, 0))
+
+    def late_constants():
+        GP(g.iota(T.imf[:], [[0, 14], [1, 16]], 0, 0, allow_small_or_imprecise_dtypes=True))
+        return GP(g.iota(T.exi[:], [[1, 14]], 0, 0))
+
+    if not is_rank:
+        g_all = late_constants()
     wait("v", "gs", g_p)
     k = V(ts(T.pm[:], T.pcol[:], 15, None, A.bitwise_and))
     wait("v", "vs", k)
@@ -156,28 +226,28 @@ def rank_program(g, core, T, topo):
         wait("v", "vs", k)
         far = [jobs[(i + rr) % n, s, rr] for rr in range(1, 5)]
         direct = [d for d in far if topo.may_write(core, d)]
-        f1, f2 = jobs[i, s, 3], jobs[i, s, 1]
+        f1, f2, f3 = jobs[i, s, 3], jobs[i, s, 1], jobs[i, s, 2]
         wait("g", "vs", k)
         trs = [(T.pk[:], T.pk[:], "pks", direct, offm)]
         if len(direct) < len(far):
             trs.append((T.pk[:], T.pkr[:], "pkrs", [f1], restm))
         send(*trs)
         wait("g", "w1s", 16)
-        send((T.w1b[:], T.wf1[:], "f1s", [f1], allm))
+        send((T.w1b[:], T.wf1[:], "f1s", [f3, f1], allm))
         wait("g", "w2s", 16)
         send((T.w2b[:], T.wf2[:], "f2s", [f2, f1], allm))
         g.sem_inc(S.gx, 1)
         wait("y", "gx", 1)
-        for c in range(0, TOK, XC):
-            g.sync.dma_start(T.xb[:, c:c + XC], T.x[:, c:c + XC]).then_inc(S.ldx, 16)
+        for c, d in zip(XC[1:], XC[2:]):
+            g.sync.dma_start(T.xb[:, c:d], T.x[:, c:d]).then_inc(S.ldx, 16)
+        g_all = late_constants()
     else:
         wait("v", "pks", bits(offm))
-    n_w = 16 if is_rank else bits(offm)
 
     def R(t, a=0, b=10):
         return t[0:HC, a:b]
 
-    u1, t1, ka, kb, vhi, r1, r2 = [R(T.fs, 10 * j, 10 * j + 10) for j in range(7)]
+    u1, t1, ka, kb, vhi, r1, r2, hp, hn = [R(T.fs, 10 * j, 10 * j + 10) for j in range(9)]
     ki, vi, tok = R(T.kv, 0, 10), R(T.kv, 10, 20), R(T.pk)
     for j in range(3):
         k = V(ts(R(T.gm, 10 * j, 10 * j + 10), tok, float(a0 + TOK * j), None, A.is_ge))
@@ -199,47 +269,57 @@ def rank_program(g, core, T, topo):
     wait("v", "vs", k)
     wait("v", "ts", t_base)
     V(ts(ka, R(T.qf, 0, 10), T.p3[0:HC, 0:1], -4097.0, A.add, A.add))
-    k_base = V(ts(kb, R(T.qf, 10, 20), T.p3[0:HC, 1:2], -3841.0, A.add, A.add))
-    wait("v", "vs", k_base)
+    k = mark["base"] = V(ts(kb, R(T.qf, 10, 20), T.p3[0:HC, 1:2], -3841.0, A.add, A.add))
+    wait("v", "vs", k)
     k = V(tt(ki, ka, kb, A.max))
     wait("v", "vs", k)
     V(ts(R(T.dq, 10, 20), ki, 15, None, A.bitwise_and))
     V(ts(R(T.dq, 0, 10), ki, 4, None, A.arith_shift_right))
-    k = V(tt(vi, t1, ki, A.subtract))
+    k = V(tt(vi, ki, t1, A.subtract))
     wait("v", "vs", k)
     k = V(ts(R(T.dq, 20, 30), vi, 63, None, A.bitwise_and))
     wait("v", "vs", k)
-    k = V(v.tensor_copy(R(T.dqf, 0, 30), R(T.dq, 0, 30)))
-    wait("v", "vs", k)
-    k_vhi = V(tt(vhi, vi, R(T.dqf, 20, 30), A.subtract))
-    wait("v", "gs", g_i32)
+    k_dq = V(v.tensor_copy(R(T.dqf, 0, 30), R(T.dq, 0, 30)))
+    wait("s", "gs", g_i32)
+    wait("s", "vs", k_dq)
     for c in range(10):
-        lh = T.lb[0:HC, 128 * c:128 * c + 128]
-        lo, hi = T.rb[0:HC, 64 * c:64 * c + 32], T.rb[0:HC, 64 * c + 32:64 * c + 64]
+        k_ab = SC(act(T.ab[0:HC, 32 * c:32 * c + 32], T.i32[0:HC, :], AF.Abs, bias=T.dqf[0:HC, c:c + 1], scale=-1.0))
+    wait("v", "vs", k_dq)
+    k = V(tt(vhi, vi, R(T.dqf, 20, 30), A.subtract))
+    wait("v", "gs", g_i32)
+    wait("v", "vs", k)
+    V(ts(hp, vhi, 0.0, None, A.max))
+    k = V(ts(hn, vhi, -1.0, 0.0, A.mult, A.min))
+    wait("s", "vs", k)
+    wait("s", "ss", k_ab)
+    k_hi = [SC(act(T.rb[0:HC, 64 * c + 32:64 * c + 64], T.ab[0:HC, 32 * c:32 * c + 32], AF.Relu,
+                   bias=T.fs[0:HC, 70 + c:71 + c], scale=T.fs[0:HC, 80 + c:81 + c])) for c in range(10)]
+    for c in range(10):
+        lh, lo = T.lb[0:HC, 128 * c:128 * c + 128], T.rb[0:HC, 64 * c:64 * c + 32]
         V(ts(lh, T.im[0:HC, :], T.dqf[0:HC, 10 + c:11 + c], None, A.is_equal))
         k = V(ts(lo, T.i32[0:HC, :], T.dqf[0:HC, c:c + 1], T.dqf[0:HC, 20 + c:21 + c], A.is_equal, A.mult))
         wait("t", "vs", k)
         PE(mm(T.p7[:, 0:32], lh, lo, False, False))
-        wait("v", "vs", k_vhi)
-        k = V(ts(hi, T.i32[0:HC, :], T.dqf[0:HC, c:c + 1], T.fs[0:HC, 40 + c:41 + c], A.is_equal, A.mult))
-        wait("t", "vs", k)
-        k = PE(mm(T.p7[:, 0:32], lh, hi, False, c == 9))
+        for d in HI.get(c, ()):
+            wait("t", "ss", k_hi[d])
+            k = PE(mm(T.p7[:, 0:32], T.lb[0:HC, 128 * d:128 * d + 128], T.rb[0:HC, 64 * d + 32:64 * d + 64], False, d == 9))
     wait("v", "ts", k)
-    k_list = V(v.tensor_copy(T.llist[:], T.p7[:, 0:32]))
-    n_l = [0, bits(allm)] + [bits(offm) // 2] * 8
+    k_list = mark["list"] = V(ts(T.llist[:], T.p7[:, 0:32], -1.0, None, A.mult))
 
     if r == 3:
-        dst = [jobs[(i + rr) % n, s, rr] for rr in (1, 4, 2, 3)]
-        if not topo.may_write(rank[i][s], dst[1]):
+        third, fourth = jobs[(i + 3) % n, s, 3], jobs[(i + 4) % n, s, 4]
+        if not topo.may_write(rank[i][s], fourth):
             wait("g", "pkrs", bits(restm))
-            send((T.pkr[:], T.pk[:], "pks", [dst[1]], offm))
+            send((T.pkr[:], T.pk[:], "pks", [fourth], offm))
         wait("g", "f1s", bits(allm))
-        send((T.wf1[:], T.w1b[:], "w1s", [dst[0]], offm))
-        send((T.wf1[:], T.w1b[:], "w1s", [dst[1]], offm))
+        send((T.wf1[:], T.w1b[:], "w1s", [fourth], offm))
         wait("g", "f2s", bits(allm))
-        send((T.wf2[:], T.w2b[:], "w2s", [dst[1]], offm))
-        send((T.wf1[:], T.w1b[:], "w1s", [dst[2]], offm))
-        send((T.wf1[:], T.w1b[:], "w1s", [dst[3]], offm))
+        send((T.wf2[:], T.w2b[:], "w2s", [fourth], offm))
+        send((T.wf1[:], T.w1b[:], "w1s", [third], offm))
+    if r == 2:
+        wait("g", "f1s", bits(allm))
+        for rr in (1, 2):
+            send((T.wf1[:], T.w1b[:], "w1s", [jobs[(i + rr) % n, s, rr]], offm))
     if r == 1:
         wait("g", "f2s", bits(allm))
         for rr in (1, 2, 3):
@@ -253,11 +333,15 @@ def rank_program(g, core, T, topo):
             trs.append((T.llist[:, 16 * x:16 * x + 16], T.lst[:, 16 * e:16 * e + 16], "l%d" % e, [rank[i][x]],
                         allm if is_rank else mk[len(trs)]))
     send(*trs)
+    if r == 4:
+        for a, q in ((T.w1b, "w1s"), (T.w2b, "w2s")):
+            wait("g", q, n_w)
+            send((a[:], a[:], q, [jobs[i, s, 5]], allm))
     for x in (0, 1):
         if relay[i][x] == core:
-            mk = split(offm, 2)
-            wait("g", "trs", bits(allm))
-            send(*[(half(T.trl, j), half(T.tin, x), "tk%d" % x, [jobs[i, (x, 1 - x)[j], 4]], mk[j]) for j in (0, 1)])
+            for sj in lates:
+                wait("g", "tr%d" % sj, bits(allm))
+                send((half(T.trl, sj), half(T.tin, x), "tk%d" % x, [doer(sj, 4, x)], offm))
 
     wait("v", "gs", g_all)
     V(ts(T.mask[:], T.imf[:], T.pmf[:], None, A.is_equal))
@@ -277,22 +361,18 @@ def rank_program(g, core, T, topo):
             o = 96 * c + 32 * j
             k = PE(mm(T.p6[:, 0:32], T.lb[0:HC, 128 * c:128 * c + 128], T.rg[0:HC, o:o + 32], c == 0 and j == 0, c == 9 and j == 2))
     wait("v", "ts", k)
-    k_gw = V(v.tensor_copy(T.gw[:], T.p6[:, 0:32]))
-    wait("v", "vs", k_gw)
+    k = mark["gw"] = V(v.tensor_copy(T.gw[:], T.p6[:, 0:32]))
+    wait("v", "vs", k)
     for x in (0, 1):
         k = V(tt(half(T.eg, x), T.gw[:, 16 * x:16 * x + 14].indirect(T.exu[:]), T.mask[:], A.mult))
     wait("t", "vs", k)
-    k = PE(mm(T.p5[:, 0:448], T.ones16[:], T.eg[0:16, :], True, True))
-    wait("s", "ts", k)
-    k_gsb = SC(g.scalar.activation(T.gsb[:], T.p5[:, 0:448], AF.Copy))
-
-    got = {}
+    k_p5 = PE(mm(T.p5[:, 0:448], T.ones16[:], T.eg[0:16, :], True, True))
 
     def lst(e):
         return T.llist[:, 16 * s:16 * s + 14] if e == 0 else T.lst[:, 16 * e:16 * e + 14]
 
     def gather(q, e):
-        wait(q, "ldx", 16 * (TOK // XC))
+        wait(q, "ldx", 16 * (len(XC) - 1))
         wait(q, "vs", k_list)
         if e:
             wait(q, "l%d" % e, n_l[e])
@@ -300,15 +380,23 @@ def rank_program(g, core, T, topo):
         if q == "v":
             got[e] = ("vs", V(v.tensor_copy(out, T.xb[:].indirect(lst(e)))))
         else:
-            got[e] = ("ss", SC(g.scalar.activation(out, T.xb[:].indirect(lst(e)), AF.Copy)))
+            got[e] = ("ss", SC(act(out, T.xb[:].indirect(lst(e)), AF.Copy)))
+
+    def send_far(sj):
+        e = place(s, sj, 4)
+        wait("g", *got[e])
+        if relay[i][s] is not None:
+            send((half(T.tks, e), half(T.trl, sj), "tr%d" % sj, [relay[i][s]], allm))
+        else:
+            send((half(T.tks, e), half(T.tin, s), "tk%d" % s, [doer(sj, 4, s)], offm))
 
     if is_rank:
-        V(v.memset(T.yb[:], 0.0))
-        for e in GATHER_V:
+        early, late = [place(s, sj, 4) for sj in lates]
+        for e in GATHER_V + [early]:
             gather("v", e)
         for e in GATHER_S:
             gather("s", e)
-        for rr in (0, 1, 2, 4, 3):
+        for rr in (0, 1, 2, 3):
             mk = split(allm, 2)
             if rr == 0:
                 wait("g", *got[1])
@@ -316,57 +404,20 @@ def rank_program(g, core, T, topo):
                 continue
             for e in (2 * rr, 2 * rr + 1):
                 wait("g", *got[e])
-            if rr == 4:
-                if relay[i][s] is not None:
-                    send((T.tks[:, 8 * 224:10 * 224], T.trl[:], "trs", [relay[i][s]], allm))
-                    continue
-                mk = split(offm, 2)
-            send(*[(half(T.tks, 2 * rr + j), half(T.tin, s), "tk%d" % s, [jobs[i, (s, 1 - s)[j], rr]], mk[j]) for j in (0, 1)])
-
-    P = [T["p%d" % b] for b in range(8)]
-    hd = {}
-
-    def layer1(b, x):
-        wait("t", "w1s", n_w)
-        if is_rank and x == s:
-            wait("t", *got[0])
-        else:
-            wait("t", "tk%d" % x, bits(allm) // 2 if r < 4 else bits(offm) // 2)
-        for f in range(FF):
-            if b and f:
-                wait("t", *([("ss", k_gsb), ("vs", k_gw)][f - 1]))
-            hd[x, f] = PE(mm(P[4 * b + f][:, 0:224], T.w1b[:, 128 * f:128 * f + 128], half(T.tin, x), True, True))
-        for f in range(FF):
-            wait("s", "ts", hd[x, f])
-            o = 672 * b + 224 * f
-            hd[x, f] = SC(g.scalar.activation(T.hid[:, o:o + 224], P[4 * b + f][:, 0:224], AF.Relu))
-
-    def layer2(b, x):
-        wait("t", "w2s", n_w)
-        wait("t", "vs", k_list if b else k_base)
-        for f in range(FF):
-            wait("t", "ss", hd[x, f])
-            o = 672 * b + 224 * f
-            k = PE(mm(P[4 * b + 3][:, 0:224], T.w2b[:, 128 * f:128 * f + 128], T.hid[:, o:o + 224], f == 0, f == 2))
-        return k
-
-    def finish(b, x, k):
-        wait("v", "ts", k)
-        wait("v", "ss", k_gsb)
-        k = V(tt(half(T.res, x), P[4 * b + 3][:, 0:224], half(T.gsb, x), A.mult))
-        if not (is_rank and x == s):
-            wait("g", "vs", k)
-            e = place(x, s, r)
-            send((half(T.res, x), half(T.rs, e), "r%d" % e, [rank[i][x]], allm if r < 4 else offm))
-        return k
+            send(*[(half(T.tks, 2 * rr + j), half(T.tin, s), "tk%d" % s, [doer((s, 1 - s)[j], rr, s)], mk[j]) for j in (0, 1)])
+    wait("s", "ts", k_p5)
+    k = mark["gsb"] = SC(act(T.gsb[:], T.p5[:, 0:448], AF.Copy))
+    if r == 4:
+        wait("g", "ss", k)
+        send((half(T.gsb, 1 - s), half(T.gsb, 1 - s), "gts", [jobs[i, s, 5]], allm))
 
     layer1(0, order[0])
-    if r == 3:
-        layer1(1, order[1])
-        for b, x in enumerate(order):
-            finish(b, x, layer2(b, x))
-    else:
-        k_self = finish(0, order[0], layer2(0, order[0]))
+    if is_rank:
+        send_far(lates[0])
+        gather("s", late)
+        send_far(lates[1])
+    k_self = finish(0, order[0], layer2(0, order[0]))
+    if r < 4:
         layer1(1, order[1])
         k = layer2(1, order[1])
         if not is_rank:
@@ -374,9 +425,11 @@ def rank_program(g, core, T, topo):
     if is_rank:
         yall = T.yb[:]
         wait("v", "vs", k_self)
+        wait("v", "ss", k_y0)
         ky = V(v.tensor_copy(yall.indirect(lst(0)), half(T.res, s)))
-        finish(1, 1 - s, k)
         for e in COMBINE[relay[i][s] is None][1:]:
+            if e == FIN:
+                finish(1, 1 - s, k)
             wait("v", "r%d" % e, bits(offm if e > 7 else allm))
             wait("v", "vs", ky)
             ky = V(tt(T.tmp[:], yall.indirect(lst(e)), half(T.rs, e), A.add))

@@ -4,8 +4,8 @@ from concourse.mybir import AluOpType, ActivationFunctionType
 TOK, FF = 4096, 3
 HC = 112
 PADC = TOK + 224
-XC = [0, 512, 2304, 4096]
-YP = 432
+XC = [0, 1024, 2560, 4096]
+YP, YS = 432, 2432
 FIN = 2
 HI = {4: (0, 1), 5: (2, 3), 6: (4, 5), 7: (6, 7), 8: (8,), 9: (9,)}
 
@@ -19,16 +19,17 @@ SCRATCH = {name: ("sbuf", [p, w], ty) for name, p, w, ty in (
     ("pm", 128, 1, I), ("pmf", 128, 1, F), ("mask", 128, 224, F), ("sel", 16, 128, B), ("padlo", 16, 32, B),
     ("padhi", 16, 32, B), ("ones", 128, 128, B), ("tri", 128, 128, B), ("ones16", 16, 128, F), ("exi", 128, 14, I),
     ("exu", 128, 14, U), ("rst", 128, 20, B), ("gm", 128, 30, B), ("m", 128, 20, B), ("scn", 128, 20, B), ("m4", 128, 20, B),
-    ("qf", 128, 20, F), ("fs", 128, 90, F), ("kv", 128, 20, I), ("dq", 128, 30, I), ("dqf", 128, 30, F), ("lb", 128, 1280, B),
-    ("ab", 128, 320, B), ("rb", 128, 640, B), ("rg", 128, 960, B), ("gb", 128, 30, B), ("gbf", 128, 30, F), ("gw", 128, 32, F),
+    ("qf", 128, 20, F), ("fs", 128, 70, F), ("kv", 128, 20, I), ("dq", 128, 30, I), ("dqf", 128, 30, F), ("lb", 128, 1280, B),
+    ("ab", 128, 320, B), ("rb", 128, 640, B), ("rg", 128, 320, F), ("lf", 128, 1280, F), ("gw", 128, 32, F),
     ("eg", 128, 448, F), ("gsb", 128, 448, F))}
 SCRATCH.update({"p%d" % b: ("psum", [128, 512], F) for b in range(8)})
 SEMAPHORES = (["ldp", "ldx", "yo", "gx", "vs", "ss", "ts", "gs", "sent", "pks", "pkrs", "w1s", "w2s", "f1s", "f2s", "tk0", "tk1",
-               "tr0", "tr1", "gts"] + ["l%d" % e for e in range(10)] + ["r%d" % e for e in range(10)])
+               "tr0", "tr1"] + ["l%d" % e for e in range(10)] + ["r%d" % e for e in range(10)])
 
-GATHER_V, GATHER_S = [0, 2, 4, 6], [1, 3, 5, 7]
-COMBINE = {True: [0, 2, 4, 1, 6, 8, 3, 5, 7, 9],
-           False: [0, 2, 4, 1, 6, 3, 5, 9, 7, 8]}
+GATHER_V, GATHER_S = [2, 0, 4, 6], [1, 3, 5, 7]
+SENDS = ((2,), (1, 4), (3, 6), (5, 7))
+COMBINE = {True: [0, 2, 1, 4, 6, 3, 5, 8, 7, 9],
+           False: [0, 2, 1, 4, 6, 3, 5, 7, 9, 8]}
 
 
 def plan(cores, topo):
@@ -66,7 +67,7 @@ def rank_program(g, core, T, topo):
     Qs = {"v": g.vector, "s": g.scalar, "t": g.tensor, "g": g, "y": g.sync}
     v, tt, ts, mm, act = g.vector, g.vector.tensor_tensor, g.vector.tensor_scalar, g.tensor.matmul, g.scalar.activation
     cnt, seen = {}, {}
-    order = [s, 1 - s]
+    order = [1 - s, s] if second else [s, 1 - s]
     lates = sorted((0, 1), key=lambda sj: relay[i][sj] is not None)
 
     def bump(sem, k=1):
@@ -123,18 +124,19 @@ def rank_program(g, core, T, topo):
     allm = topo.mask(rank[0][0], rank[0][1])
     offm = topo.mask(rank[0][0], rank[1][0])
     restm = allm & ~offm
-    n_w = 16 if is_rank else bits(allm) if second else bits(offm)
-    n_l = [0, bits(allm)] + [bits(offm) // 2] * 8
+    n_w1 = 16 if is_rank else bits(allm if second else offm)
+    n_w2 = 16 if is_rank else bits(allm if r == 4 and not second else offm)
+    n_l = [0, bits(allm)] + [bits(offm) // 2] * 6 + [bits(offm)] * 2
 
     P = [T["p%d" % b] for b in range(8)]
     hd, got, mark = {}, {}, {}
 
     def layer1(b, x):
-        wait("t", "w1s", n_w)
+        wait("t", "w1s", n_w1)
         if is_rank and x == s:
             wait("t", *got[0])
         else:
-            wait("t", "tk%d" % x, bits(allm) // 2 if r < 4 else bits(offm))
+            wait("t", "tk%d" % x, bits(offm) if r == 4 else bits(allm) // (1 if r == 1 and x == s else 2))
         for f in range(FF):
             if b and f:
                 wait("t", *([("ss", mark["gsb"]), ("vs", mark["gw"])][f - 1]))
@@ -145,9 +147,8 @@ def rank_program(g, core, T, topo):
             hd[x, f] = SC(act(T.hid[:, o:o + 224], P[4 * b + f][:, 0:224], AF.Relu))
 
     def layer2(b, x):
-        wait("t", "w2s", n_w)
-        if not second:
-            wait("t", "vs", mark["list"] if b else mark["base"])
+        wait("t", "w2s", n_w2)
+        wait("t", "vs", mark["list"] if b else mark["base"])
         for f in range(FF):
             wait("t", "ss", hd[x, f])
             o = 672 * b + 224 * f
@@ -156,23 +157,13 @@ def rank_program(g, core, T, topo):
 
     def finish(b, x, k):
         wait("v", "ts", k)
-        if second:
-            wait("v", "gts", bits(allm))
-        else:
-            wait("v", "ss", mark["gsb"])
+        wait("v", "ss", mark["gsb"])
         k = V(tt(half(T.res, x), P[4 * b + 3][:, 0:224], half(T.gsb, x), A.mult))
         if not (is_rank and x == s):
             wait("g", "vs", k)
             e = place(x, s, r)
             send((half(T.res, x), half(T.rs, e), "r%d" % e, [rank[i][x]], allm if r < 4 else offm))
         return k
-
-    if second:
-        layer1(0, 1 - s)
-        finish(0, 1 - s, layer2(0, 1 - s))
-        for sem in ("vs", "ss", "ts", "sent"):
-            wait("g", sem)
-        return
 
     if is_rank:
         g.sync.dma_start(T.picki[0:HC, :], T.pick[:]).then_inc(S.ldp, 16)
@@ -194,8 +185,8 @@ def rank_program(g, core, T, topo):
         k = V(v.memset(T.yb[:, 0:YP], 0.0))
         wait("s", "vs", k)
         c = YP
-        while c < PADC:
-            w = min(c, PADC - c)
+        while c < YS:
+            w = min(c, YS - c)
             k_y0 = SC(act(T.yb[:, c:c + w], T.yb[:, 0:w], AF.Copy))
             wait("s", "ss", k_y0)
             c += w
@@ -241,13 +232,14 @@ def rank_program(g, core, T, topo):
         for c, d in zip(XC[1:], XC[2:]):
             g.sync.dma_start(T.xb[:, c:d], T.x[:, c:d]).then_inc(S.ldx, 16)
         g_all = late_constants()
+        g_y0 = GP(g.iota(T.yb[:, YS:PADC], [[0, PADC - YS]], 0, 0, allow_small_or_imprecise_dtypes=True))
     else:
-        wait("v", "pks", bits(offm))
+        wait("v", "pks", bits(allm if second else offm))
 
     def R(t, a=0, b=10):
         return t[0:HC, a:b]
 
-    u1, t1, ka, kb, vhi, r1, r2, hp, hn = [R(T.fs, 10 * j, 10 * j + 10) for j in range(9)]
+    u1, t1, ka, kb, vhi, hp, hn = [R(T.fs, 10 * j, 10 * j + 10) for j in range(7)]
     ki, vi, tok = R(T.kv, 0, 10), R(T.kv, 10, 20), R(T.pk)
     for j in range(3):
         k = V(ts(R(T.gm, 10 * j, 10 * j + 10), tok, float(a0 + TOK * j), None, A.is_ge))
@@ -293,29 +285,33 @@ def rank_program(g, core, T, topo):
     wait("s", "vs", k)
     wait("s", "ss", k_ab)
     k_hi = [SC(act(T.rb[0:HC, 64 * c + 32:64 * c + 64], T.ab[0:HC, 32 * c:32 * c + 32], AF.Relu,
-                   bias=T.fs[0:HC, 70 + c:71 + c], scale=T.fs[0:HC, 80 + c:81 + c])) for c in range(10)]
+                   bias=T.fs[0:HC, 50 + c:51 + c], scale=T.fs[0:HC, 60 + c:61 + c])) for c in range(10)]
+    k_lh = []
     for c in range(10):
         lh, lo = T.lb[0:HC, 128 * c:128 * c + 128], T.rb[0:HC, 64 * c:64 * c + 32]
-        V(ts(lh, T.im[0:HC, :], T.dqf[0:HC, 10 + c:11 + c], None, A.is_equal))
+        k_lh.append(V(ts(lh, T.im[0:HC, :], T.dqf[0:HC, 10 + c:11 + c], None, A.is_equal)))
         k = V(ts(lo, T.i32[0:HC, :], T.dqf[0:HC, c:c + 1], T.dqf[0:HC, 20 + c:21 + c], A.is_equal, A.mult))
         wait("t", "vs", k)
         PE(mm(T.p7[:, 0:32], lh, lo, False, False))
         for d in HI.get(c, ()):
             wait("t", "ss", k_hi[d])
             k = PE(mm(T.p7[:, 0:32], T.lb[0:HC, 128 * d:128 * d + 128], T.rb[0:HC, 64 * d + 32:64 * d + 64], False, d == 9))
+    for c in (0, 5):
+        wait("s", "vs", k_lh[c + 4])
+        k_lf = SC(act(T.lf[0:HC, 128 * c:128 * c + 640], T.lb[0:HC, 128 * c:128 * c + 640], AF.Copy))
     wait("v", "ts", k)
     k_list = mark["list"] = V(ts(T.llist[:], T.p7[:, 0:32], -1.0, None, A.mult))
 
     if r == 3:
-        third, fourth = jobs[(i + 3) % n, s, 3], jobs[(i + 4) % n, s, 4]
+        fourth = jobs[(i + 4) % n, s, 4]
         if not topo.may_write(rank[i][s], fourth):
             wait("g", "pkrs", bits(restm))
             send((T.pkr[:], T.pk[:], "pks", [fourth], offm))
         wait("g", "f1s", bits(allm))
         send((T.wf1[:], T.w1b[:], "w1s", [fourth], offm))
         wait("g", "f2s", bits(allm))
-        send((T.wf2[:], T.w2b[:], "w2s", [fourth], offm))
-        send((T.wf1[:], T.w1b[:], "w1s", [third], offm))
+        send((T.wf2[:], T.w2b[:], "w2s", [jobs[(i + 4) % n, s, 5]], offm))
+        send((T.wf1[:], T.wf1[:], "f1s", [jobs[(i + 3) % n, s, 5]], offm))
     if r == 2:
         wait("g", "f1s", bits(allm))
         for rr in (1, 2):
@@ -324,19 +320,29 @@ def rank_program(g, core, T, topo):
         wait("g", "f2s", bits(allm))
         for rr in (1, 2, 3):
             send((T.wf2[:], T.w2b[:], "w2s", [jobs[(i + rr) % n, s, rr]], offm))
-    wait("g", "vs", k_list)
-    mk = split(offm if r == 4 else restm, 2)
+    if r == 4 and not second:
+        wait("g", "pks", bits(offm))
+        send((T.pk[:], T.pk[:], "pks", [jobs[i, s, 5]], allm))
+    mk = split(restm, 2)
     trs = []
     for x in order:
         e = place(x, s, r)
-        if e:
+        if e and not second:
+            wait("g", "vs", k_list)
             trs.append((T.llist[:, 16 * x:16 * x + 16], T.lst[:, 16 * e:16 * e + 16], "l%d" % e, [rank[i][x]],
-                        allm if is_rank else mk[len(trs)]))
-    send(*trs)
+                        allm if is_rank else offm if r == 4 else mk[len(trs)]))
     if r == 4:
-        for a, q in ((T.w1b, "w1s"), (T.w2b, "w2s")):
-            wait("g", q, n_w)
-            send((a[:], a[:], q, [jobs[i, s, 5]], allm))
+        for t in sorted(trs, key=lambda t: topo.may_write(t[3][0], core)):
+            send(t)
+    else:
+        send(*trs)
+    if r == 4:
+        a, q, c = (T.w2b, "w2s", 4) if second else (T.w1b, "w1s", 5)
+        wait("g", q, bits(offm))
+        send((a[:], a[:], q, [jobs[i, s, c]], allm))
+    if second:
+        wait("g", "f1s", bits(offm))
+        send((T.wf1[:], T.w1b[:], "w1s", [jobs[i, s, 3]], offm))
     for x in (0, 1):
         if relay[i][x] == core:
             for sj in lates:
@@ -344,22 +350,15 @@ def rank_program(g, core, T, topo):
                 send((half(T.trl, sj), half(T.tin, x), "tk%d" % x, [doer(sj, 4, x)], offm))
 
     wait("v", "gs", g_all)
+    for c in range(10):
+        rg = T.rg[0:HC, 32 * c:32 * c + 32]
+        k = V(ts(rg, T.i32[0:HC, :], T.dqf[0:HC, c:c + 1], T.pk[0:HC, 10 + c:11 + c], A.is_equal, A.mult))
+        wait("t", "vs", k)
+        if c == 0:
+            wait("t", "ss", k_lf)
+        k = PE(mm(T.p6[:, 0:32], T.lf[0:HC, 128 * c:128 * c + 128], rg, c == 0, c == 9))
     V(ts(T.mask[:], T.imf[:], T.pmf[:], None, A.is_equal))
     V(v.tensor_copy(T.exu[:], T.exi[:]))
-    gate, g1, g2, g3 = R(T.pk, 10, 20), R(T.gb, 0, 10), R(T.gb, 10, 20), R(T.gb, 20, 30)
-    for out, a, b in ((g1, gate, None), (r1, gate, g1), (g2, r1, None), (r2, r1, g2), (g3, r2, None),
-                      (R(T.gbf, 0, 30), R(T.gb, 0, 30), None)):
-        k = V(v.tensor_copy(out, a) if b is None else tt(out, a, b, A.subtract))
-        wait("v", "vs", k)
-    for c in range(10):
-        for j in range(3):
-            o = 96 * c + 32 * j
-            k = V(ts(T.rg[0:HC, o:o + 32], T.i32[0:HC, :], T.dqf[0:HC, c:c + 1], T.gbf[0:HC, 10 * j + c:10 * j + c + 1],
-                     A.is_equal, A.mult))
-        wait("t", "vs", k)
-        for j in range(3):
-            o = 96 * c + 32 * j
-            k = PE(mm(T.p6[:, 0:32], T.lb[0:HC, 128 * c:128 * c + 128], T.rg[0:HC, o:o + 32], c == 0 and j == 0, c == 9 and j == 2))
     wait("v", "ts", k)
     k = mark["gw"] = V(v.tensor_copy(T.gw[:], T.p6[:, 0:32]))
     wait("v", "vs", k)
@@ -396,20 +395,14 @@ def rank_program(g, core, T, topo):
             gather("v", e)
         for e in GATHER_S:
             gather("s", e)
-        for rr in (0, 1, 2, 3):
-            mk = split(allm, 2)
-            if rr == 0:
-                wait("g", *got[1])
-                send((half(T.tks, 1), half(T.tin, s), "tk%d" % s, [rank[i][1 - s]], mk[0]))
-                continue
-            for e in (2 * rr, 2 * rr + 1):
+        for es in SENDS:
+            for e in es:
                 wait("g", *got[e])
-            send(*[(half(T.tks, 2 * rr + j), half(T.tin, s), "tk%d" % s, [doer((s, 1 - s)[j], rr, s)], mk[j]) for j in (0, 1)])
+            mk = split(allm, len(es))
+            send(*[(half(T.tks, e), half(T.tin, s), "tk%d" % s, [doer(s if e % 2 == 0 else 1 - s, e // 2, s)], m)
+                   for e, m in zip(es, mk)])
     wait("s", "ts", k_p5)
     k = mark["gsb"] = SC(act(T.gsb[:], T.p5[:, 0:448], AF.Copy))
-    if r == 4:
-        wait("g", "ss", k)
-        send((half(T.gsb, 1 - s), half(T.gsb, 1 - s), "gts", [jobs[i, s, 5]], allm))
 
     layer1(0, order[0])
     if is_rank:
@@ -426,6 +419,7 @@ def rank_program(g, core, T, topo):
         yall = T.yb[:]
         wait("v", "vs", k_self)
         wait("v", "ss", k_y0)
+        wait("v", "gs", g_y0)
         ky = V(v.tensor_copy(yall.indirect(lst(0)), half(T.res, s)))
         for e in COMBINE[relay[i][s] is None][1:]:
             if e == FIN:

from concourse.bass import DstId, RemoteDMATransfer
from concourse.mybir import AluOpType, ActivationFunctionType

TOK, FF = 4096, 3
HC = 112
PADC = TOK + 224
XC = [0, 1024, 2560, 4096]
YP, YS = 432, 2432
FIN = 2
HI = {4: (0, 1), 5: (2, 3), 6: (4, 5), 7: (6, 7), 8: (8,), 9: (9,)}

F, B, I, U = "float32", "bfloat16", "int32", "uint16"
SCRATCH = {name: ("sbuf", [p, w], ty) for name, p, w, ty in (
    ("picki", 128, 10, I), ("gatef", 128, 10, F), ("pk", 128, 20, F), ("pkr", 128, 20, F),
    ("w1b", 128, 384, F), ("w2b", 128, 384, F), ("wf1", 128, 384, F), ("wf2", 128, 384, F),
    ("xb", 128, PADC, F), ("yb", 128, PADC, F), ("tks", 128, 2240, F), ("tin", 128, 448, F), ("trl", 128, 448, F),
    ("hid", 128, 1344, F), ("res", 128, 448, F), ("rs", 128, 2240, F), ("tmp", 128, 224, F), ("lst", 128, 160, U),
    ("llist", 128, 32, U), ("im", 128, 128, B), ("i32", 128, 32, B), ("imf", 128, 224, F), ("pcol", 128, 1, I),
    ("pm", 128, 1, I), ("pmf", 128, 1, F), ("mask", 128, 224, F), ("sel", 16, 128, B), ("padlo", 16, 32, B),
    ("padhi", 16, 32, B), ("ones", 128, 128, B), ("tri", 128, 128, B), ("ones16", 16, 128, F), ("exi", 128, 14, I),
    ("exu", 128, 14, U), ("rst", 128, 20, B), ("gm", 128, 30, B), ("m", 128, 20, B), ("scn", 128, 20, B), ("m4", 128, 20, B),
    ("qf", 128, 20, F), ("fs", 128, 70, F), ("kv", 128, 20, I), ("dq", 128, 30, I), ("dqf", 128, 30, F), ("lb", 128, 1280, B),
    ("ab", 128, 320, B), ("rb", 128, 640, B), ("rg", 128, 320, F), ("lf", 128, 1280, F), ("gw", 128, 32, F),
    ("eg", 128, 448, F), ("gsb", 128, 448, F))}
SCRATCH.update({"p%d" % b: ("psum", [128, 512], F) for b in range(8)})
SEMAPHORES = (["ldp", "ldx", "yo", "gx", "vs", "ss", "ts", "gs", "sent", "pks", "pkrs", "w1s", "w2s", "f1s", "f2s", "tk0", "tk1",
               "tr0", "tr1"] + ["l%d" % e for e in range(10)] + ["r%d" % e for e in range(10)])

GATHER_V, GATHER_S = [2, 0, 4, 6], [1, 3, 5, 7]
SENDS = ((2,), (1, 4), (3, 6), (5, 7))
COMBINE = {True: [0, 2, 1, 4, 6, 3, 5, 8, 7, 9],
           False: [0, 2, 1, 4, 6, 3, 5, 7, 9, 8]}


def plan(cores, topo):
    sims = range(80)
    chips = []
    for c in cores:
        if topo.chip(c) not in chips:
            chips.append(topo.chip(c))
    rank = [[c for c in cores if topo.chip(c) == ch] for ch in chips]
    relay, jobs = [], {}
    for i, ch in enumerate(chips):
        mcore = [c for c in sims if topo.mates(ch, topo.chip(c))]
        relay.append([])
        for s in (0, 1):
            rc = rank[i][s]
            h = [c for c in sims if topo.chip(c) == ch and topo.die(c) == topo.die(rc) and c != rc]
            h.sort(key=lambda c: (topo.may_write(c, mcore[0]), c))
            back = [c for c in mcore if topo.die(c) == topo.die(rc) and topo.may_write(c, rc)]
            relay[i].append(None if topo.may_write(rc, mcore[0]) else h[1])
            for r, c in enumerate([rc] + h[:3] + back[:2]):
                jobs[i, s, r] = c
    return rank, relay, jobs, len(chips)


def rank_program(g, core, T, topo):
    A, AF, S = AluOpType, ActivationFunctionType, T.sem
    rank, relay, jobs, n = plan(T.cores, topo)
    mine = [k for k in jobs if jobs[k] == core]
    if not mine:
        return
    i, s, r = mine[0]
    is_rank, second = r == 0, r == 5
    r = min(r, 4)
    a0 = TOK * T.cores.index(rank[i][0])
    Qs = {"v": g.vector, "s": g.scalar, "t": g.tensor, "g": g, "y": g.sync}
    v, tt, ts, mm, act = g.vector, g.vector.tensor_tensor, g.vector.tensor_scalar, g.tensor.matmul, g.scalar.activation
    cnt, seen = {}, {}
    order = [1 - s, s] if second else [s, 1 - s]
    lates = sorted((0, 1), key=lambda sj: relay[i][sj] is not None)

    def bump(sem, k=1):
        cnt[sem] = cnt.get(sem, 0) + k
        return cnt[sem]

    def wait(q, sem, val=None):
        val = cnt.get(sem, 0) if val is None else val
        if seen.get((q, sem), 0) < val:
            Qs[q].wait_ge(S[sem], val)
            seen[q, sem] = val

    def V(ins):
        ins.then_inc(S.vs, 1)
        return bump("vs")

    def SC(ins):
        ins.then_inc(S.ss, 1)
        return bump("ss")

    def PE(ins):
        ins.then_inc(S.ts, 1)
        return bump("ts")

    def GP(ins):
        ins.then_inc(S.gs, 1)
        return bump("gs")

    def bits(mask):
        return bin(mask).count("1")

    def split(mask, k):
        b = [e for e in range(16) if mask >> e & 1]
        w = len(b) // k
        return [sum(1 << e for e in b[j * w:(j + 1) * w]) for j in range(k)]

    def send(*trs):
        out = []
        for src, dst, sem, dsts, mask in trs:
            ids = [DstId(rid=topo.addr(d)[0], pnc=topo.addr(d)[1]) for d in dsts]
            out.append(RemoteDMATransfer(dst_ids=ids, dma_engine_mask=mask, remote_sem=S[sem], srcs=[src], dsts=[dst] * len(ids)))
            bump("sent", bits(mask))
        g.remote_dma_fused(out, local_sem=S.sent)

    def place(x, sj, rr):
        return 2 * rr + (1 if sj != x else 0)

    def doer(sj, rr, x):
        return jobs[i, sj, rr if rr < 4 or x == sj else 5]

    def half(t, x, w=224):
        return t[:, w * x:w * x + w]

    allm = topo.mask(rank[0][0], rank[0][1])
    offm = topo.mask(rank[0][0], rank[1][0])
    restm = allm & ~offm
    n_w1 = 16 if is_rank else bits(allm if second else offm)
    n_w2 = 16 if is_rank else bits(allm if r == 4 and not second else offm)
    n_l = [0, bits(allm)] + [bits(offm) // 2] * 6 + [bits(offm)] * 2

    P = [T["p%d" % b] for b in range(8)]
    hd, got, mark = {}, {}, {}

    def layer1(b, x):
        wait("t", "w1s", n_w1)
        if is_rank and x == s:
            wait("t", *got[0])
        else:
            wait("t", "tk%d" % x, bits(offm) if r == 4 else bits(allm) // (1 if r == 1 and x == s else 2))
        for f in range(FF):
            if b and f:
                wait("t", *([("ss", mark["gsb"]), ("vs", mark["gw"])][f - 1]))
            hd[x, f] = PE(mm(P[4 * b + f][:, 0:224], T.w1b[:, 128 * f:128 * f + 128], half(T.tin, x), True, True))
        for f in range(FF):
            wait("s", "ts", hd[x, f])
            o = 672 * b + 224 * f
            hd[x, f] = SC(act(T.hid[:, o:o + 224], P[4 * b + f][:, 0:224], AF.Relu))

    def layer2(b, x):
        wait("t", "w2s", n_w2)
        wait("t", "vs", mark["list"] if b else mark["base"])
        for f in range(FF):
            wait("t", "ss", hd[x, f])
            o = 672 * b + 224 * f
            k = PE(mm(P[4 * b + 3][:, 0:224], T.w2b[:, 128 * f:128 * f + 128], T.hid[:, o:o + 224], f == 0, f == 2))
        return k

    def finish(b, x, k):
        wait("v", "ts", k)
        wait("v", "ss", mark["gsb"])
        k = V(tt(half(T.res, x), P[4 * b + 3][:, 0:224], half(T.gsb, x), A.mult))
        if not (is_rank and x == s):
            wait("g", "vs", k)
            e = place(x, s, r)
            send((half(T.res, x), half(T.rs, e), "r%d" % e, [rank[i][x]], allm if r < 4 else offm))
        return k

    if is_rank:
        g.sync.dma_start(T.picki[0:HC, :], T.pick[:]).then_inc(S.ldp, 16)
        g.scalar.dma_start(T.gatef[0:HC, :], T.gate[:]).then_inc(S.ldp, 16)
        g.sync.dma_start(T.picki[HC:128, :], T.pick[:, 0:10]).then_inc(S.ldp, 16)
        g.scalar.dma_start(T.gatef[HC:128, :], T.gate[:, 0:10]).then_inc(S.ldp, 16)
        g.sync.dma_start(T.w1b[:], T.w1[:]).then_inc(S.w1s, 16)
        g.sync.dma_start(T.w2b[:], T.w2[:]).then_inc(S.w2s, 16)
        g.sync.dma_start(T.xb[:, XC[0]:XC[1]], T.x[:, XC[0]:XC[1]]).then_inc(S.ldx, 16)

    c_ones = V(v.memset(T.ones[:], 1.0))
    c_rst = V(v.memset(T.rst[:], 1.0))
    V(v.memset(T.padhi[:], -float(TOK)))
    V(v.memset(T.ones16[:], 1.0))
    wait("v", "vs", c_rst)
    V(v.memset(T.rst[:, 10:11], 0.0))
    if is_rank:
        V(v.memset(T.xb[:, TOK:PADC], 0.0))
        k = V(v.memset(T.yb[:, 0:YP], 0.0))
        wait("s", "vs", k)
        c = YP
        while c < YS:
            w = min(c, YS - c)
            k_y0 = SC(act(T.yb[:, c:c + w], T.yb[:, 0:w], AF.Copy))
            wait("s", "ss", k_y0)
            c += w
    GP(g.iota(T.im[:], [[0, 8], [1, 16]], 0, 0, allow_small_or_imprecise_dtypes=True))
    g_p = GP(g.iota(T.pcol[:], [[0, 1]], 0, 1))
    GP(g.iota(T.padlo[:], [[0, 2], [-16, 16]], 0, -1, allow_small_or_imprecise_dtypes=True))
    wait("g", "vs", c_ones)
    g_tri = GP(g.affine_select(T.tri[:], T.ones[:], [[1, 128]], A.is_gt, 0.0, 0, -1))
    g_i32 = GP(g.iota(T.i32[:], [[1, 32]], 0, 0, allow_small_or_imprecise_dtypes=True))

    def late_constants():
        GP(g.iota(T.imf[:], [[0, 14], [1, 16]], 0, 0, allow_small_or_imprecise_dtypes=True))
        return GP(g.iota(T.exi[:], [[1, 14]], 0, 0))

    if not is_rank:
        g_all = late_constants()
    wait("v", "gs", g_p)
    k = V(ts(T.pm[:], T.pcol[:], 15, None, A.bitwise_and))
    wait("v", "vs", k)
    k = V(v.tensor_copy(T.pmf[:], T.pm[:]))
    wait("v", "vs", k)
    V(ts(T.sel[:], T.im[0:16, :], T.pmf[0:16, :], None, A.is_equal))

    if is_rank:
        wait("v", "ldp", 64)
        V(v.tensor_copy(T.pk[:, 0:10], T.picki[:]))
        k = V(v.tensor_copy(T.pk[:, 10:20], T.gatef[:]))
        wait("v", "vs", k)
        far = [jobs[(i + rr) % n, s, rr] for rr in range(1, 5)]
        direct = [d for d in far if topo.may_write(core, d)]
        f1, f2, f3 = jobs[i, s, 3], jobs[i, s, 1], jobs[i, s, 2]
        wait("g", "vs", k)
        trs = [(T.pk[:], T.pk[:], "pks", direct, offm)]
        if len(direct) < len(far):
            trs.append((T.pk[:], T.pkr[:], "pkrs", [f1], restm))
        send(*trs)
        wait("g", "w1s", 16)
        send((T.w1b[:], T.wf1[:], "f1s", [f3, f1], allm))
        wait("g", "w2s", 16)
        send((T.w2b[:], T.wf2[:], "f2s", [f2, f1], allm))
        g.sem_inc(S.gx, 1)
        wait("y", "gx", 1)
        for c, d in zip(XC[1:], XC[2:]):
            g.sync.dma_start(T.xb[:, c:d], T.x[:, c:d]).then_inc(S.ldx, 16)
        g_all = late_constants()
        g_y0 = GP(g.iota(T.yb[:, YS:PADC], [[0, PADC - YS]], 0, 0, allow_small_or_imprecise_dtypes=True))
    else:
        wait("v", "pks", bits(allm if second else offm))

    def R(t, a=0, b=10):
        return t[0:HC, a:b]

    u1, t1, ka, kb, vhi, hp, hn = [R(T.fs, 10 * j, 10 * j + 10) for j in range(7)]
    ki, vi, tok = R(T.kv, 0, 10), R(T.kv, 10, 20), R(T.pk)
    for j in range(3):
        k = V(ts(R(T.gm, 10 * j, 10 * j + 10), tok, float(a0 + TOK * j), None, A.is_ge))
    wait("v", "vs", k)
    k = V(tt(R(T.m, 0, 20), R(T.gm, 0, 20), R(T.gm, 10, 30), A.subtract))
    wait("v", "vs", k)
    k_scn = V(v.tensor_tensor_scan(R(T.scn, 0, 20), R(T.rst, 0, 20), R(T.m, 0, 20), 0.0, A.mult, A.add))
    wait("t", "gs", g_tri)
    wait("t", "vs", k_scn)
    t_base = PE(mm(T.p3[0:HC, 0:2], T.tri[0:HC, 0:HC], T.scn[0:HC, 9:20:10], True, True))
    PE(mm(T.p7[:, 0:32], T.sel[:], T.padhi[:], True, False))
    PE(mm(T.p7[:, 0:32], T.sel[:], T.padlo[:], False, False))
    k_m4 = V(ts(R(T.m4, 0, 20), R(T.m, 0, 20), 4096.0, None, A.mult))
    V(ts(u1, R(T.gm, 10, 20), -3840.0, float(-(a0 + TOK)), A.mult, A.add))
    wait("v", "vs", k_m4)
    V(tt(R(T.qf, 0, 20), R(T.scn, 0, 20), R(T.m4, 0, 20), A.add))
    wait("v", "vs", k_m4 + 1)
    k = V(tt(t1, tok, u1, A.add))
    wait("v", "vs", k)
    wait("v", "ts", t_base)
    V(ts(ka, R(T.qf, 0, 10), T.p3[0:HC, 0:1], -4097.0, A.add, A.add))
    k = mark["base"] = V(ts(kb, R(T.qf, 10, 20), T.p3[0:HC, 1:2], -3841.0, A.add, A.add))
    wait("v", "vs", k)
    k = V(tt(ki, ka, kb, A.max))
    wait("v", "vs", k)
    V(ts(R(T.dq, 10, 20), ki, 15, None, A.bitwise_and))
    V(ts(R(T.dq, 0, 10), ki, 4, None, A.arith_shift_right))
    k = V(tt(vi, ki, t1, A.subtract))
    wait("v", "vs", k)
    k = V(ts(R(T.dq, 20, 30), vi, 63, None, A.bitwise_and))
    wait("v", "vs", k)
    k_dq = V(v.tensor_copy(R(T.dqf, 0, 30), R(T.dq, 0, 30)))
    wait("s", "gs", g_i32)
    wait("s", "vs", k_dq)
    for c in range(10):
        k_ab = SC(act(T.ab[0:HC, 32 * c:32 * c + 32], T.i32[0:HC, :], AF.Abs, bias=T.dqf[0:HC, c:c + 1], scale=-1.0))
    wait("v", "vs", k_dq)
    k = V(tt(vhi, vi, R(T.dqf, 20, 30), A.subtract))
    wait("v", "gs", g_i32)
    wait("v", "vs", k)
    V(ts(hp, vhi, 0.0, None, A.max))
    k = V(ts(hn, vhi, -1.0, 0.0, A.mult, A.min))
    wait("s", "vs", k)
    wait("s", "ss", k_ab)
    k_hi = [SC(act(T.rb[0:HC, 64 * c + 32:64 * c + 64], T.ab[0:HC, 32 * c:32 * c + 32], AF.Relu,
                   bias=T.fs[0:HC, 50 + c:51 + c], scale=T.fs[0:HC, 60 + c:61 + c])) for c in range(10)]
    k_lh = []
    for c in range(10):
        lh, lo = T.lb[0:HC, 128 * c:128 * c + 128], T.rb[0:HC, 64 * c:64 * c + 32]
        k_lh.append(V(ts(lh, T.im[0:HC, :], T.dqf[0:HC, 10 + c:11 + c], None, A.is_equal)))
        k = V(ts(lo, T.i32[0:HC, :], T.dqf[0:HC, c:c + 1], T.dqf[0:HC, 20 + c:21 + c], A.is_equal, A.mult))
        wait("t", "vs", k)
        PE(mm(T.p7[:, 0:32], lh, lo, False, False))
        for d in HI.get(c, ()):
            wait("t", "ss", k_hi[d])
            k = PE(mm(T.p7[:, 0:32], T.lb[0:HC, 128 * d:128 * d + 128], T.rb[0:HC, 64 * d + 32:64 * d + 64], False, d == 9))
    for c in (0, 5):
        wait("s", "vs", k_lh[c + 4])
        k_lf = SC(act(T.lf[0:HC, 128 * c:128 * c + 640], T.lb[0:HC, 128 * c:128 * c + 640], AF.Copy))
    wait("v", "ts", k)
    k_list = mark["list"] = V(ts(T.llist[:], T.p7[:, 0:32], -1.0, None, A.mult))

    if r == 3:
        fourth = jobs[(i + 4) % n, s, 4]
        if not topo.may_write(rank[i][s], fourth):
            wait("g", "pkrs", bits(restm))
            send((T.pkr[:], T.pk[:], "pks", [fourth], offm))
        wait("g", "f1s", bits(allm))
        send((T.wf1[:], T.w1b[:], "w1s", [fourth], offm))
        wait("g", "f2s", bits(allm))
        send((T.wf2[:], T.w2b[:], "w2s", [jobs[(i + 4) % n, s, 5]], offm))
        send((T.wf1[:], T.wf1[:], "f1s", [jobs[(i + 3) % n, s, 5]], offm))
    if r == 2:
        wait("g", "f1s", bits(allm))
        for rr in (1, 2):
            send((T.wf1[:], T.w1b[:], "w1s", [jobs[(i + rr) % n, s, rr]], offm))
    if r == 1:
        wait("g", "f2s", bits(allm))
        for rr in (1, 2, 3):
            send((T.wf2[:], T.w2b[:], "w2s", [jobs[(i + rr) % n, s, rr]], offm))
    if r == 4 and not second:
        wait("g", "pks", bits(offm))
        send((T.pk[:], T.pk[:], "pks", [jobs[i, s, 5]], allm))
    mk = split(restm, 2)
    trs = []
    for x in order:
        e = place(x, s, r)
        if e and not second:
            wait("g", "vs", k_list)
            trs.append((T.llist[:, 16 * x:16 * x + 16], T.lst[:, 16 * e:16 * e + 16], "l%d" % e, [rank[i][x]],
                        allm if is_rank else offm if r == 4 else mk[len(trs)]))
    if r == 4:
        for t in sorted(trs, key=lambda t: topo.may_write(t[3][0], core)):
            send(t)
    else:
        send(*trs)
    if r == 4:
        a, q, c = (T.w2b, "w2s", 4) if second else (T.w1b, "w1s", 5)
        wait("g", q, bits(offm))
        send((a[:], a[:], q, [jobs[i, s, c]], allm))
    if second:
        wait("g", "f1s", bits(offm))
        send((T.wf1[:], T.w1b[:], "w1s", [jobs[i, s, 3]], offm))
    for x in (0, 1):
        if relay[i][x] == core:
            for sj in lates:
                wait("g", "tr%d" % sj, bits(allm))
                send((half(T.trl, sj), half(T.tin, x), "tk%d" % x, [doer(sj, 4, x)], offm))

    wait("v", "gs", g_all)
    for c in range(10):
        rg = T.rg[0:HC, 32 * c:32 * c + 32]
        k = V(ts(rg, T.i32[0:HC, :], T.dqf[0:HC, c:c + 1], T.pk[0:HC, 10 + c:11 + c], A.is_equal, A.mult))
        wait("t", "vs", k)
        if c == 0:
            wait("t", "ss", k_lf)
        k = PE(mm(T.p6[:, 0:32], T.lf[0:HC, 128 * c:128 * c + 128], rg, c == 0, c == 9))
    V(ts(T.mask[:], T.imf[:], T.pmf[:], None, A.is_equal))
    V(v.tensor_copy(T.exu[:], T.exi[:]))
    wait("v", "ts", k)
    k = mark["gw"] = V(v.tensor_copy(T.gw[:], T.p6[:, 0:32]))
    wait("v", "vs", k)
    for x in (0, 1):
        k = V(tt(half(T.eg, x), T.gw[:, 16 * x:16 * x + 14].indirect(T.exu[:]), T.mask[:], A.mult))
    wait("t", "vs", k)
    k_p5 = PE(mm(T.p5[:, 0:448], T.ones16[:], T.eg[0:16, :], True, True))

    def lst(e):
        return T.llist[:, 16 * s:16 * s + 14] if e == 0 else T.lst[:, 16 * e:16 * e + 14]

    def gather(q, e):
        wait(q, "ldx", 16 * (len(XC) - 1))
        wait(q, "vs", k_list)
        if e:
            wait(q, "l%d" % e, n_l[e])
        out = half(T.tks, e) if e else half(T.tin, s)
        if q == "v":
            got[e] = ("vs", V(v.tensor_copy(out, T.xb[:].indirect(lst(e)))))
        else:
            got[e] = ("ss", SC(act(out, T.xb[:].indirect(lst(e)), AF.Copy)))

    def send_far(sj):
        e = place(s, sj, 4)
        wait("g", *got[e])
        if relay[i][s] is not None:
            send((half(T.tks, e), half(T.trl, sj), "tr%d" % sj, [relay[i][s]], allm))
        else:
            send((half(T.tks, e), half(T.tin, s), "tk%d" % s, [doer(sj, 4, s)], offm))

    if is_rank:
        early, late = [place(s, sj, 4) for sj in lates]
        for e in GATHER_V + [early]:
            gather("v", e)
        for e in GATHER_S:
            gather("s", e)
        for es in SENDS:
            for e in es:
                wait("g", *got[e])
            mk = split(allm, len(es))
            send(*[(half(T.tks, e), half(T.tin, s), "tk%d" % s, [doer(s if e % 2 == 0 else 1 - s, e // 2, s)], m)
                   for e, m in zip(es, mk)])
    wait("s", "ts", k_p5)
    k = mark["gsb"] = SC(act(T.gsb[:], T.p5[:, 0:448], AF.Copy))

    layer1(0, order[0])
    if is_rank:
        send_far(lates[0])
        gather("s", late)
        send_far(lates[1])
    k_self = finish(0, order[0], layer2(0, order[0]))
    if r < 4:
        layer1(1, order[1])
        k = layer2(1, order[1])
        if not is_rank:
            finish(1, order[1], k)
    if is_rank:
        yall = T.yb[:]
        wait("v", "vs", k_self)
        wait("v", "ss", k_y0)
        wait("v", "gs", g_y0)
        ky = V(v.tensor_copy(yall.indirect(lst(0)), half(T.res, s)))
        for e in COMBINE[relay[i][s] is None][1:]:
            if e == FIN:
                finish(1, 1 - s, k)
            wait("v", "r%d" % e, bits(offm if e > 7 else allm))
            wait("v", "vs", ky)
            ky = V(tt(T.tmp[:], yall.indirect(lst(e)), half(T.rs, e), A.add))
            wait("v", "vs", ky)
            ky = V(v.tensor_copy(yall.indirect(lst(e)), T.tmp[:]))
        for q in ("y", "s"):
            wait(q, "vs", ky)
        g.sync.dma_start(T.y[:, 0:2048], T.yb[:, 0:2048]).then_inc(S.yo, 16)
        g.scalar.dma_start(T.y[:, 2048:4096], T.yb[:, 2048:4096]).then_inc(S.yo, 16)
        wait("g", "yo", 32)
    for sem in ("vs", "ss", "ts", "gs", "sent"):
        wait("g", sem)
